import numpy as np
import ml_dtypes


def mxq(x, axis, fmt="e4m3"):
    dtype, down = {"e4m3": (ml_dtypes.float8_e4m3fn, 7), "e5m2": (ml_dtypes.float8_e5m2, 14)}[fmt]
    v = np.moveaxis(np.asarray(x, np.float32).astype(ml_dtypes.bfloat16).astype(np.float64), axis, -1)
    blocks = v.reshape(v.shape[:-1] + (-1, 32))
    amax = np.abs(blocks).max(-1, keepdims=True)
    byte = np.maximum(np.where(amax > 0, np.frexp(amax)[1] - 1 + 127, 0) - down, 1)
    scale = np.exp2(byte - 127.0)
    codes = (blocks / scale).astype(np.float32).astype(dtype).astype(np.float64)
    return np.moveaxis((codes * scale).reshape(v.shape), -1, axis)


WIDE = False


def mx_kscale(k):
    if not WIDE:
        return np.ones(k)
    levels = np.array([10, -10, 5, -5, 0])
    if k % 512:
        return np.exp2(np.random.permutation(np.resize(levels, k // 32))).repeat(32)
    a = np.empty((k // 512, 16))
    for p in range(k // 512):
        a[p, :8] = np.random.permutation(np.resize(levels, 8))
        for g in range(8):
            far = levels[np.abs(levels - a[p, g]) >= 10]
            a[p, g + 8] = far[np.random.randint(len(far))]
    return np.exp2(a.ravel()).repeat(32)


def f64(x):
    return np.asarray(x).astype(np.float64)


def striped(idx):
    return np.tile(np.asarray(idx).reshape(-1, 16).T, (8, 1)).astype(np.uint16)


def unstriped(offs):
    return offs[:16].T.reshape(-1).astype(np.int64)


E2M1 = np.array([0.0, 0.5, 1.0, 1.5, 2.0, 3.0, 4.0, 6.0, -0.0, -0.5, -1.0, -1.5, -2.0, -3.0, -4.0, -6.0])


def pack_weight(w, fmt):
    k, n = w.shape
    w = f64(np.asarray(w, np.float32).astype(ml_dtypes.bfloat16)).reshape(k // 32, 32, n)
    amax = np.abs(w).max(1)
    if fmt == "e4m3":
        byte = np.frexp(amax)[1] - 1 + 127 - 7
    else:
        mant, ex = np.frexp(amax / 6.0)
        byte = np.where(mant > 0.5, ex, ex - 1) + 127
    byte = np.clip(np.where(amax > 0, byte, 1), 1, 254)
    scaled = (w * np.exp2(127.0 - byte)[:, None, :]).reshape(k, n).astype(np.float32)
    by_word = np.ascontiguousarray(scaled.reshape(k // 512, 128, 4, n).transpose(0, 1, 3, 2))
    if fmt == "e4m3":
        words = by_word.astype(ml_dtypes.float8_e4m3fn).view(np.uint8)
    else:
        c = by_word.astype(ml_dtypes.float4_e2m1fn).view(np.uint8) & 0xF
        words = (c[..., 0::2] | (c[..., 1::2] << 4)).reshape(k // 512, 128, 2 * n)
    return np.ascontiguousarray(words), np.ascontiguousarray(byte.astype(np.uint8).reshape(k // 512, 16, n))


def unpack_weight(words, scales, fmt):
    g, _, n = scales.shape
    words = np.ascontiguousarray(words).reshape(g, 128, n, -1)
    if fmt == "e4m3":
        vals = words.view(ml_dtypes.float8_e4m3fn).astype(np.float64)
    else:
        nib = np.empty((g, 128, n, 4), np.uint8)
        nib[..., 0::2] = words & 0xF
        nib[..., 1::2] = words >> 4
        vals = E2M1[nib]
    vals = vals * np.repeat(np.exp2(scales.astype(np.float64) - 127.0), 8, axis=1)[..., None]
    return vals.transpose(0, 1, 3, 2).reshape(g * 512, n)


D, T, I, G, U, Q = 512, 4096, 1024, 64, 512, 128


def setup_inputs():
    n = np.random.standard_normal
    idx = np.random.permutation(T)[:I]
    idx2 = np.random.permutation(U)[:G]
    fd = mx_kscale(D)
    keysp = pack_weight(n((D, T)) / fd[:, None], "e4m3")
    return {
        "query": (n((D, Q)) * 1.0 / np.sqrt(D) * fd[:, None]).astype(np.float32),
        "keys_words": keysp[0],
        "keys_scales": keysp[1],
        "pquery": (n((D, Q)) * 1.0 / np.sqrt(D) * fd[:, None]).astype(np.float32),
        "pgsum": (n((D, U)) / fd[:, None]).astype(np.float32),
        "offs": striped(idx),
        "offs2": striped(idx2),
    }


def reference(query, keys_words, keys_scales, pquery, pgsum, offs, offs2):
    idx = unstriped(offs)
    idx2 = unstriped(offs2)
    keysu = unpack_weight(keys_words, keys_scales, "e4m3")
    queryq = mxq(f64(query), 0, "e4m3")
    keysidxg = keysu[:, idx]
    a = queryq.T @ keysidxg
    r = np.log(np.exp(a).reshape(Q, G, I // G).sum(axis=2))
    rf = np.zeros((Q, U))
    rf[:, idx2] = r
    pqueryq = mxq(f64(pquery), 0, "e4m3")
    pgsumq = mxq(f64(pgsum), 0, "e4m3")
    b = pqueryq.T @ pgsumq
    y = b + rf
    return y

@@ -1,0 +1,151 @@
+from contextlib import ExitStack
+
+import concourse.mybir as mybir
+
+D, T, SLOTS, PAGES, U, Q = 512, 4096, 1024, 64, 512, 128
+FLOPS = 2 * D * Q * (SLOTS + U)
+
+F32 = mybir.dt.float32
+BF16 = mybir.dt.bfloat16
+I32 = mybir.dt.int32
+U32 = mybir.dt.uint32
+U16 = mybir.dt.uint16
+U8 = mybir.dt.uint8
+FP8X4 = mybir.dt.float8_e4m3fn_x4
+ALU = mybir.AluOpType
+ACT = mybir.ActivationFunctionType
+AX = mybir.AxisListType
+
+P = 128
+PACK = 4
+PAGE = SLOTS // PAGES
+CHUNK = 512
+CHUNKS = SLOTS // CHUNK
+CHUNK_PAGES = CHUNK // PAGE
+HALF = U // 2
+
+
+def load_rows(nc, pool, src, name):
+    width = src.shape[1]
+    raw = pool.tile([P, PACK, width], F32, name=name)
+    nc.sync.dma_start(out=raw[:], in_=src.rearrange("(p t) c -> p t c", t=PACK))
+    return raw
+
+
+def interleave(nc, grouped, raw):
+    nc.scalar.copy(
+        out=grouped.rearrange("p (c i) t -> p c t i", i=4),
+        in_=raw[:].rearrange("p t (c i) -> p c t i", i=4),
+    )
+
+
+def quantise(nc, pool, grouped, name):
+    width = grouped.shape[1]
+    codes = pool.tile([P, width], U32, name=name + "_codes", align_bytes=64)
+    scales = pool.tile([P, width], U8, name=name + "_scales", align_bytes=64)
+    nc.vector.quantize_mx(
+        out=codes[:].bitcast(FP8X4), scales=scales[:], in_=grouped[:].rearrange("p c t -> p (c t)")
+    )
+    return codes, scales
+
+
+def tile_attend_pagelogsum_kernel(tc, query, keys_words, keys_scales, pquery, pgsum, offs, offs2, out):
+    nc = tc.nc
+    with ExitStack() as ctx:
+        pool = ctx.enter_context(tc.tile_pool(name="held", bufs=1))
+        psum = ctx.enter_context(tc.psum_pool(name="psum", bufs=1))
+
+        slot_list = pool.tile([P, SLOTS // 16], U16, name="slot_list")
+        nc.sync.dma_start(slot_list[:], offs)
+
+        pool_scales = pool.tile([P, T], U8, name="pool_scales", align_bytes=64)
+        nc.vector.memset(pool_scales[:].bitcast(I32), 0)
+        for r in range(4):
+            nc.scalar.dma_start(
+                out=pool_scales[r:P:32, :].bitcast(I32), in_=keys_scales[0][r:16:4, :].bitcast(I32)
+            )
+
+        q_raw = load_rows(nc, pool, query, "q_raw")
+        pool_words = pool.tile([P, T], U32, name="pool_words", align_bytes=64)
+        nc.sync.dma_start(
+            out=pool_words[:].bitcast(I32), in_=keys_words[0].rearrange("p n t -> p (n t)").bitcast(I32)
+        )
+        pq_raw = load_rows(nc, pool, pquery, "pq_raw")
+        pg_raw = [load_rows(nc, pool, pgsum[:, h * HALF : (h + 1) * HALF], f"pg_raw{h}") for h in range(2)]
+        page_list = pool.tile([P, PAGES // 16], U16, name="page_list")
+        nc.sync.dma_start(page_list[:], offs2)
+
+        placed = pool.tile([P, U], F32, name="placed")
+        nc.gpsimd.memset(placed[:], 0.0)
+
+        q_bf = pool.tile([P, Q, PACK], BF16, name="q_bf", align_bytes=64)
+        interleave(nc, q_bf[:], q_raw)
+        key_scales = pool.tile([P, SLOTS], U8, name="key_scales", align_bytes=64)
+        nc.vector.tensor_copy(key_scales[:], pool_scales[:].indirect(slot_list[:]))
+        q_codes, q_scales = quantise(nc, pool, q_bf, "q")
+
+        scores = []
+        for c in range(CHUNKS):
+            key_words = pool.tile([P, CHUNK], U32, name=f"key_words{c}", align_bytes=64)
+            cols = slice(c * CHUNK // 16, (c + 1) * CHUNK // 16)
+            nc.vector.tensor_copy(key_words[:], pool_words[:].indirect(slot_list[:, cols]))
+            bank = psum.tile([P, CHUNK], F32, name=f"scores{c}")
+            nc.tensor.matmul_mx(
+                out=bank[:],
+                lhsT=q_codes[:].bitcast(FP8X4),
+                lhsT_scale=q_scales[:],
+                rhs=key_words[:].bitcast(FP8X4),
+                rhs_scale=key_scales[:, c * CHUNK : (c + 1) * CHUNK],
+                start=True,
+                stop=True,
+            )
+            scores.append(bank)
+
+        pq_bf = pool.tile([P, Q, PACK], BF16, name="pq_bf", align_bytes=64)
+        interleave(nc, pq_bf[:], pq_raw)
+        pg_bf = pool.tile([P, U, PACK], BF16, name="pg_bf", align_bytes=64)
+        for h in range(2):
+            interleave(nc, pg_bf[:, h * HALF : (h + 1) * HALF, :], pg_raw[h])
+
+        top = pool.tile([P, PAGES], F32, name="top")
+        total = pool.tile([P, PAGES], F32, name="total")
+        powers = []
+        for c in range(CHUNKS):
+            pages = slice(c * CHUNK_PAGES, (c + 1) * CHUNK_PAGES)
+            by_page = scores[c][:].rearrange("p (g j) -> p g j", j=PAGE)
+            nc.vector.tensor_reduce(out=top[:, pages], in_=by_page, axis=AX.X, op=ALU.max)
+            shifted = pool.tile([P, CHUNK_PAGES, PAGE], F32, name=f"shifted{c}")
+            nc.vector.tensor_tensor(
+                out=shifted[:],
+                in0=by_page,
+                in1=top[:, pages].unsqueeze(2).to_broadcast([P, CHUNK_PAGES, PAGE]),
+                op=ALU.subtract,
+            )
+            power = pool.tile([P, CHUNK_PAGES, PAGE], F32, name=f"power{c}")
+            nc.scalar.activation(out=power[:], in_=shifted[:], func=ACT.Exp)
+            powers.append(power)
+
+        nc.vector.tensor_reduce(out=total[:, 0:CHUNK_PAGES], in_=powers[0][:], axis=AX.X, op=ALU.add)
+        pq_codes, pq_scales = quantise(nc, pool, pq_bf, "pq")
+        nc.vector.tensor_reduce(out=total[:, CHUNK_PAGES:PAGES], in_=powers[1][:], axis=AX.X, op=ALU.add)
+        pg_codes, pg_scales = quantise(nc, pool, pg_bf, "pg")
+        summary = psum.tile([P, U], F32, name="summary")
+        nc.tensor.matmul_mx(
+            out=summary[:],
+            lhsT=pq_codes[:].bitcast(FP8X4),
+            lhsT_scale=pq_scales[:],
+            rhs=pg_codes[:].bitcast(FP8X4),
+            rhs_scale=pg_scales[:],
+            start=True,
+            stop=True,
+        )
+
+        logs = pool.tile([P, PAGES], F32, name="logs")
+        nc.scalar.activation(out=logs[:], in_=total[:], func=ACT.Ln)
+        nc.vector.tensor_tensor(placed[:].indirect(page_list[:]), logs[:], top[:], ALU.add)
+
+        for h, queue in enumerate((nc.sync, nc.scalar)):
+            cols = slice(h * HALF, (h + 1) * HALF)
+            result = pool.tile([P, HALF], F32, name=f"result{h}")
+            nc.vector.tensor_tensor(out=result[:], in0=summary[:, cols], in1=placed[:, cols], op=ALU.add)
+            queue.dma_start(out=out[:, cols], in_=result[:])

@@ -23,6 +23,10 @@ CHUNK = 512
 CHUNKS = SLOTS // CHUNK
 CHUNK_PAGES = CHUNK // PAGE
 HALF = U // 2
+HEAD = 768
+PIECE = 256
+PIECES = SLOTS // PIECE
+PIECE_PAGES = PIECE // PAGE
 
 
 def load_rows(nc, pool, src, name):
@@ -55,21 +59,19 @@ def tile_attend_pagelogsum_kernel(tc, query, keys_words, keys_scales, pquery, pg
         pool = ctx.enter_context(tc.tile_pool(name="held", bufs=1))
         psum = ctx.enter_context(tc.psum_pool(name="psum", bufs=1))
 
-        slot_list = pool.tile([P, SLOTS // 16], U16, name="slot_list")
-        nc.sync.dma_start(slot_list[:], offs)
-
         pool_scales = pool.tile([P, T], U8, name="pool_scales", align_bytes=64)
         nc.vector.memset(pool_scales[:].bitcast(I32), 0)
+        q_raw = load_rows(nc, pool, query, "q_raw")
+        slot_list = pool.tile([P, SLOTS // 16], U16, name="slot_list")
+        nc.sync.dma_start(slot_list[:], offs)
+        pool_words = pool.tile([P, T], U32, name="pool_words", align_bytes=64)
+        words_in = keys_words[0].rearrange("p n t -> p (n t)").bitcast(I32)
+        nc.sync.dma_start(out=pool_words[:, 0:HEAD].bitcast(I32), in_=words_in[:, 0:HEAD])
         for r in range(4):
-            nc.scalar.dma_start(
+            nc.sync.dma_start(
                 out=pool_scales[r:P:32, :].bitcast(I32), in_=keys_scales[0][r:16:4, :].bitcast(I32)
             )
-
-        q_raw = load_rows(nc, pool, query, "q_raw")
-        pool_words = pool.tile([P, T], U32, name="pool_words", align_bytes=64)
-        nc.sync.dma_start(
-            out=pool_words[:].bitcast(I32), in_=keys_words[0].rearrange("p n t -> p (n t)").bitcast(I32)
-        )
+        nc.sync.dma_start(out=pool_words[:, HEAD:T].bitcast(I32), in_=words_in[:, HEAD:T])
         pq_raw = load_rows(nc, pool, pquery, "pq_raw")
         pg_raw = [load_rows(nc, pool, pgsum[:, h * HALF : (h + 1) * HALF], f"pg_raw{h}") for h in range(2)]
         page_list = pool.tile([P, PAGES // 16], U16, name="page_list")
@@ -111,24 +113,33 @@ def tile_attend_pagelogsum_kernel(tc, query, keys_words, keys_scales, pquery, pg
         total = pool.tile([P, PAGES], F32, name="total")
         powers = []
         for c in range(CHUNKS):
-            pages = slice(c * CHUNK_PAGES, (c + 1) * CHUNK_PAGES)
-            by_page = scores[c][:].rearrange("p (g j) -> p g j", j=PAGE)
-            nc.vector.tensor_reduce(out=top[:, pages], in_=by_page, axis=AX.X, op=ALU.max)
-            shifted = pool.tile([P, CHUNK_PAGES, PAGE], F32, name=f"shifted{c}")
-            nc.vector.tensor_tensor(
-                out=shifted[:],
-                in0=by_page,
-                in1=top[:, pages].unsqueeze(2).to_broadcast([P, CHUNK_PAGES, PAGE]),
-                op=ALU.subtract,
-            )
+            halves = range(CHUNK // PIECE)
+            by_page = [
+                scores[c][:, h * PIECE : (h + 1) * PIECE].rearrange("p (g j) -> p g j", j=PAGE) for h in halves
+            ]
+            tops = [
+                top[:, c * CHUNK_PAGES + h * PIECE_PAGES : c * CHUNK_PAGES + (h + 1) * PIECE_PAGES] for h in halves
+            ]
             power = pool.tile([P, CHUNK_PAGES, PAGE], F32, name=f"power{c}")
-            nc.scalar.activation(out=power[:], in_=shifted[:], func=ACT.Exp)
+            for h in halves:
+                nc.vector.tensor_reduce(out=tops[h], in_=by_page[h], axis=AX.X, op=ALU.max)
+            for h in halves:
+                shifted = pool.tile([P, PIECE_PAGES, PAGE], F32, name=f"shifted{c}{h}")
+                nc.vector.tensor_tensor(
+                    out=shifted[:],
+                    in0=by_page[h],
+                    in1=tops[h].unsqueeze(2).to_broadcast([P, PIECE_PAGES, PAGE]),
+                    op=ALU.subtract,
+                )
+                nc.scalar.activation(
+                    out=power[:, h * PIECE_PAGES : (h + 1) * PIECE_PAGES, :], in_=shifted[:], func=ACT.Exp
+                )
             powers.append(power)
 
         nc.vector.tensor_reduce(out=total[:, 0:CHUNK_PAGES], in_=powers[0][:], axis=AX.X, op=ALU.add)
         pq_codes, pq_scales = quantise(nc, pool, pq_bf, "pq")
-        nc.vector.tensor_reduce(out=total[:, CHUNK_PAGES:PAGES], in_=powers[1][:], axis=AX.X, op=ALU.add)
         pg_codes, pg_scales = quantise(nc, pool, pg_bf, "pg")
+        nc.vector.tensor_reduce(out=total[:, CHUNK_PAGES:PAGES], in_=powers[1][:], axis=AX.X, op=ALU.add)
         summary = psum.tile([P, U], F32, name="summary")
         nc.tensor.matmul_mx(
             out=summary[:],

@@ -91,64 +91,88 @@ def tile_attend_pagelogsum_kernel(tc, query, keys_words, keys_scales, pquery, pg
             key_words = pool.tile([P, CHUNK], U32, name=f"key_words{c}", align_bytes=64)
             cols = slice(c * CHUNK // 16, (c + 1) * CHUNK // 16)
             nc.vector.tensor_copy(key_words[:], pool_words[:].indirect(slot_list[:, cols]))
-            bank = psum.tile([P, CHUNK], F32, name=f"scores{c}")
-            nc.tensor.matmul_mx(
-                out=bank[:],
-                lhsT=q_codes[:].bitcast(FP8X4),
-                lhsT_scale=q_scales[:],
-                rhs=key_words[:].bitcast(FP8X4),
-                rhs_scale=key_scales[:, c * CHUNK : (c + 1) * CHUNK],
-                start=True,
-                stop=True,
-            )
-            scores.append(bank)
+            for h in range(CHUNK // PIECE):
+                bank = psum.tile([P, PIECE], F32, name=f"scores{c}{h}")
+                nc.tensor.matmul_mx(
+                    out=bank[:],
+                    lhsT=q_codes[:].bitcast(FP8X4),
+                    lhsT_scale=q_scales[:],
+                    rhs=key_words[:, h * PIECE : (h + 1) * PIECE].bitcast(FP8X4),
+                    rhs_scale=key_scales[:, c * CHUNK + h * PIECE : c * CHUNK + (h + 1) * PIECE],
+                    start=True,
+                    stop=True,
+                )
+                scores.append(bank[:].rearrange("p (g j) -> p g j", j=PAGE))
 
         pq_bf = pool.tile([P, Q, PACK], BF16, name="pq_bf", align_bytes=64)
         interleave(nc, pq_bf[:], pq_raw)
-        pg_bf = pool.tile([P, U, PACK], BF16, name="pg_bf", align_bytes=64)
-        for h in range(2):
-            interleave(nc, pg_bf[:, h * HALF : (h + 1) * HALF, :], pg_raw[h])
+        pg_bf = [pool.tile([P, HALF, PACK], BF16, name=f"pg_bf{h}", align_bytes=64) for h in range(2)]
+        interleave(nc, pg_bf[0][:], pg_raw[0])
+        nc.gpsimd.tensor_scalar(
+            out=pg_bf[1][:],
+            in0=pg_raw[1][:].rearrange("p t c -> p c t"),
+            scalar1=1.0,
+            scalar2=0.0,
+            op0=ALU.mult,
+            op1=ALU.add,
+        )
 
         top = pool.tile([P, PAGES], F32, name="top")
         total = pool.tile([P, PAGES], F32, name="total")
-        powers = []
-        for c in range(CHUNKS):
-            halves = range(CHUNK // PIECE)
-            by_page = [
-                scores[c][:, h * PIECE : (h + 1) * PIECE].rearrange("p (g j) -> p g j", j=PAGE) for h in halves
-            ]
-            tops = [
-                top[:, c * CHUNK_PAGES + h * PIECE_PAGES : c * CHUNK_PAGES + (h + 1) * PIECE_PAGES] for h in halves
-            ]
-            power = pool.tile([P, CHUNK_PAGES, PAGE], F32, name=f"power{c}")
-            for h in halves:
-                nc.vector.tensor_reduce(out=tops[h], in_=by_page[h], axis=AX.X, op=ALU.max)
-            for h in halves:
-                shifted = pool.tile([P, PIECE_PAGES, PAGE], F32, name=f"shifted{c}{h}")
-                nc.vector.tensor_tensor(
-                    out=shifted[:],
-                    in0=by_page[h],
-                    in1=tops[h].unsqueeze(2).to_broadcast([P, PIECE_PAGES, PAGE]),
-                    op=ALU.subtract,
-                )
-                nc.scalar.activation(
-                    out=power[:, h * PIECE_PAGES : (h + 1) * PIECE_PAGES, :], in_=shifted[:], func=ACT.Exp
-                )
-            powers.append(power)
+        power = pool.tile([P, PAGES, PAGE], F32, name="power")
+        minus_top = pool.tile([P, PIECE_PAGES], F32, name="minus_top")
 
-        nc.vector.tensor_reduce(out=total[:, 0:CHUNK_PAGES], in_=powers[0][:], axis=AX.X, op=ALU.add)
+        def pages(n):
+            return slice(n * PIECE_PAGES, (n + 1) * PIECE_PAGES)
+
+        def find_top(n):
+            nc.vector.tensor_reduce(out=top[:, pages(n)], in_=scores[n], axis=AX.X, op=ALU.max)
+
+        def exponentials(n):
+            shifted = pool.tile([P, PIECE_PAGES, PAGE], F32, name=f"shifted{n}")
+            nc.vector.tensor_tensor(
+                out=shifted[:],
+                in0=scores[n],
+                in1=top[:, pages(n)].unsqueeze(2).to_broadcast([P, PIECE_PAGES, PAGE]),
+                op=ALU.subtract,
+            )
+            nc.scalar.activation(out=power[:, pages(n), :], in_=shifted[:], func=ACT.Exp)
+
+        nc.vector.tensor_reduce(out=minus_top[:], in_=scores[0], axis=AX.X, op=ALU.max, negate=True)
+        for g in range(PIECE_PAGES):
+            nc.scalar.activation(
+                out=power[:, g, :], in_=scores[0][:, g, :], func=ACT.Exp, bias=minus_top[:, g : g + 1]
+            )
+        find_top(1)
+        find_top(2)
+        exponentials(1)
+        find_top(3)
+        exponentials(2)
+        exponentials(3)
+        nc.vector.tensor_scalar(
+            out=top[:, pages(0)], in0=minus_top[:], scalar1=-1.0, scalar2=None, op0=ALU.mult
+        )
+
+        nc.vector.tensor_reduce(
+            out=total[:, 0:CHUNK_PAGES], in_=power[:, 0:CHUNK_PAGES, :], axis=AX.X, op=ALU.add
+        )
         pq_codes, pq_scales = quantise(nc, pool, pq_bf, "pq")
-        pg_codes, pg_scales = quantise(nc, pool, pg_bf, "pg")
-        nc.vector.tensor_reduce(out=total[:, CHUNK_PAGES:PAGES], in_=powers[1][:], axis=AX.X, op=ALU.add)
-        summary = psum.tile([P, U], F32, name="summary")
-        nc.tensor.matmul_mx(
-            out=summary[:],
-            lhsT=pq_codes[:].bitcast(FP8X4),
-            lhsT_scale=pq_scales[:],
-            rhs=pg_codes[:].bitcast(FP8X4),
-            rhs_scale=pg_scales[:],
-            start=True,
-            stop=True,
+        summary = []
+        for h in range(2):
+            pg_codes, pg_scales = quantise(nc, pool, pg_bf[h], f"pg{h}")
+            bank = psum.tile([P, HALF], F32, name=f"summary{h}")
+            nc.tensor.matmul_mx(
+                out=bank[:],
+                lhsT=pq_codes[:].bitcast(FP8X4),
+                lhsT_scale=pq_scales[:],
+                rhs=pg_codes[:].bitcast(FP8X4),
+                rhs_scale=pg_scales[:],
+                start=True,
+                stop=True,
+            )
+            summary.append(bank)
+        nc.vector.tensor_reduce(
+            out=total[:, CHUNK_PAGES:PAGES], in_=power[:, CHUNK_PAGES:PAGES, :], axis=AX.X, op=ALU.add
         )
 
         logs = pool.tile([P, PAGES], F32, name="logs")
@@ -158,5 +182,5 @@ def tile_attend_pagelogsum_kernel(tc, query, keys_words, keys_scales, pquery, pg
         for h, queue in enumerate((nc.sync, nc.scalar)):
             cols = slice(h * HALF, (h + 1) * HALF)
             result = pool.tile([P, HALF], F32, name=f"result{h}")
-            nc.vector.tensor_tensor(out=result[:], in0=summary[:, cols], in1=placed[:, cols], op=ALU.add)
+            nc.vector.tensor_tensor(out=result[:], in0=summary[h][:], in1=placed[:, cols], op=ALU.add)
             queue.dma_start(out=out[:, cols], in_=result[:])

@@ -23,15 +23,15 @@ CHUNK = 512
 CHUNKS = SLOTS // CHUNK
 CHUNK_PAGES = CHUNK // PAGE
 HALF = U // 2
-HEAD = 768
+HEAD = 1280
 PIECE = 256
 PIECES = SLOTS // PIECE
 PIECE_PAGES = PIECE // PAGE
 
 
-def load_rows(nc, pool, src, name):
+def load_rows(nc, pool, src, name, tag=None):
     width = src.shape[1]
-    raw = pool.tile([P, PACK, width], F32, name=name)
+    raw = pool.tile([P, PACK, width], F32, name=name, tag=tag or name, align_bytes=64)
     nc.sync.dma_start(out=raw[:], in_=src.rearrange("(p t) c -> p t c", t=PACK))
     return raw
 
@@ -61,7 +61,6 @@ def tile_attend_pagelogsum_kernel(tc, query, keys_words, keys_scales, pquery, pg
 
         pool_scales = pool.tile([P, T], U8, name="pool_scales", align_bytes=64)
         nc.vector.memset(pool_scales[:].bitcast(I32), 0)
-        q_raw = load_rows(nc, pool, query, "q_raw")
         slot_list = pool.tile([P, SLOTS // 16], U16, name="slot_list")
         nc.sync.dma_start(slot_list[:], offs)
         pool_words = pool.tile([P, T], U32, name="pool_words", align_bytes=64)
@@ -72,8 +71,9 @@ def tile_attend_pagelogsum_kernel(tc, query, keys_words, keys_scales, pquery, pg
                 out=pool_scales[r:P:32, :].bitcast(I32), in_=keys_scales[0][r:16:4, :].bitcast(I32)
             )
         nc.sync.dma_start(out=pool_words[:, HEAD:T].bitcast(I32), in_=words_in[:, HEAD:T])
-        pq_raw = load_rows(nc, pool, pquery, "pq_raw")
+        q_raw = load_rows(nc, pool, query, "q_raw", "key_words1")
         pg_raw = [load_rows(nc, pool, pgsum[:, h * HALF : (h + 1) * HALF], f"pg_raw{h}") for h in range(2)]
+        pq_raw = load_rows(nc, pool, pquery, "pq_raw")
         page_list = pool.tile([P, PAGES // 16], U16, name="page_list")
         nc.sync.dma_start(page_list[:], offs2)
 
@@ -84,13 +84,14 @@ def tile_attend_pagelogsum_kernel(tc, query, keys_words, keys_scales, pquery, pg
         interleave(nc, q_bf[:], q_raw)
         key_scales = pool.tile([P, SLOTS], U8, name="key_scales", align_bytes=64)
         nc.vector.tensor_copy(key_scales[:], pool_scales[:].indirect(slot_list[:]))
-        q_codes, q_scales = quantise(nc, pool, q_bf, "q")
 
         scores = []
         for c in range(CHUNKS):
-            key_words = pool.tile([P, CHUNK], U32, name=f"key_words{c}", align_bytes=64)
+            key_words = pool.tile([P, CHUNK], U32, name=f"key_words{c}", tag=f"key_words{c}", align_bytes=64)
             cols = slice(c * CHUNK // 16, (c + 1) * CHUNK // 16)
             nc.vector.tensor_copy(key_words[:], pool_words[:].indirect(slot_list[:, cols]))
+            if c == 0:
+                q_codes, q_scales = quantise(nc, pool, q_bf, "q")
             for h in range(CHUNK // PIECE):
                 bank = psum.tile([P, PIECE], F32, name=f"scores{c}{h}")
                 nc.tensor.matmul_mx(
@@ -105,17 +106,17 @@ def tile_attend_pagelogsum_kernel(tc, query, keys_words, keys_scales, pquery, pg
                 scores.append(bank[:].rearrange("p (g j) -> p g j", j=PAGE))
 
         pq_bf = pool.tile([P, Q, PACK], BF16, name="pq_bf", align_bytes=64)
-        interleave(nc, pq_bf[:], pq_raw)
         pg_bf = [pool.tile([P, HALF, PACK], BF16, name=f"pg_bf{h}", align_bytes=64) for h in range(2)]
         interleave(nc, pg_bf[0][:], pg_raw[0])
-        nc.gpsimd.tensor_scalar(
-            out=pg_bf[1][:],
-            in0=pg_raw[1][:].rearrange("p t c -> p c t"),
-            scalar1=1.0,
-            scalar2=0.0,
-            op0=ALU.mult,
-            op1=ALU.add,
-        )
+        for grouped, raw in ((pg_bf[1], pg_raw[1]), (pq_bf, pq_raw)):
+            nc.gpsimd.tensor_scalar(
+                out=grouped[:],
+                in0=raw[:].rearrange("p t c -> p c t"),
+                scalar1=1.0,
+                scalar2=0.0,
+                op0=ALU.mult,
+                op1=ALU.add,
+            )
 
         top = pool.tile([P, PAGES], F32, name="top")
         total = pool.tile([P, PAGES], F32, name="total")
@@ -157,6 +158,9 @@ def tile_attend_pagelogsum_kernel(tc, query, keys_words, keys_scales, pquery, pg
             out=total[:, 0:CHUNK_PAGES], in_=power[:, 0:CHUNK_PAGES, :], axis=AX.X, op=ALU.add
         )
         pq_codes, pq_scales = quantise(nc, pool, pq_bf, "pq")
+        nc.vector.tensor_reduce(
+            out=total[:, CHUNK_PAGES:PAGES], in_=power[:, CHUNK_PAGES:PAGES, :], axis=AX.X, op=ALU.add
+        )
         summary = []
         for h in range(2):
             pg_codes, pg_scales = quantise(nc, pool, pg_bf[h], f"pg{h}")
@@ -171,9 +175,6 @@ def tile_attend_pagelogsum_kernel(tc, query, keys_words, keys_scales, pquery, pg
                 stop=True,
             )
             summary.append(bank)
-        nc.vector.tensor_reduce(
-            out=total[:, CHUNK_PAGES:PAGES], in_=power[:, CHUNK_PAGES:PAGES, :], axis=AX.X, op=ALU.add
-        )
 
         logs = pool.tile([P, PAGES], F32, name="logs")
         nc.scalar.activation(out=logs[:], in_=total[:], func=ACT.Ln)

@@ -2,8 +2,8 @@ from contextlib import ExitStack
 
 import concourse.mybir as mybir
 
-D, T, SLOTS, PAGES, U, Q = 512, 4096, 1024, 64, 512, 128
-FLOPS = 2 * D * Q * (SLOTS + U)
+D, TOKENS, SLOTS, PAGES, ALL_PAGES, ROWS = 512, 4096, 1024, 64, 512, 128
+FLOPS = 2 * D * ROWS * (SLOTS + ALL_PAGES)
 
 F32 = mybir.dt.float32
 BF16 = mybir.dt.bfloat16
@@ -18,15 +18,17 @@ AX = mybir.AxisListType
 
 P = 128
 PACK = 4
+LIST_ROWS = 16
+QUADRANT = 32
+SCALE_ROWS = 4
+LINE = 4
 PAGE = SLOTS // PAGES
 CHUNK = 512
-CHUNKS = SLOTS // CHUNK
 CHUNK_PAGES = CHUNK // PAGE
-HALF = U // 2
-HEAD = 1280
 PIECE = 256
-PIECES = SLOTS // PIECE
 PIECE_PAGES = PIECE // PAGE
+HALF = ALL_PAGES // 2
+HEAD = 1280
 
 
 def load_rows(nc, pool, src, name, tag=None):
@@ -36,10 +38,21 @@ def load_rows(nc, pool, src, name, tag=None):
     return raw
 
 
-def interleave(nc, grouped, raw):
+def interleave_on_scalar(nc, grouped, raw):
     nc.scalar.copy(
-        out=grouped.rearrange("p (c i) t -> p c t i", i=4),
-        in_=raw[:].rearrange("p t (c i) -> p c t i", i=4),
+        out=grouped[:].rearrange("p (c i) t -> p c t i", i=LINE),
+        in_=raw[:].rearrange("p t (c i) -> p c t i", i=LINE),
+    )
+
+
+def interleave_on_gpsimd(nc, grouped, raw):
+    nc.gpsimd.tensor_scalar(
+        out=grouped[:],
+        in0=raw[:].rearrange("p t c -> p c t"),
+        scalar1=1.0,
+        scalar2=0.0,
+        op0=ALU.mult,
+        op1=ALU.add,
     )
 
 
@@ -53,70 +66,79 @@ def quantise(nc, pool, grouped, name):
     return codes, scales
 
 
+def multiply(nc, bank, row_codes, row_scales, codes, scales):
+    nc.tensor.matmul_mx(
+        out=bank[:],
+        lhsT=row_codes[:].bitcast(FP8X4),
+        lhsT_scale=row_scales[:],
+        rhs=codes.bitcast(FP8X4),
+        rhs_scale=scales,
+        start=True,
+        stop=True,
+    )
+
+
 def tile_attend_pagelogsum_kernel(tc, query, keys_words, keys_scales, pquery, pgsum, offs, offs2, out):
     nc = tc.nc
     with ExitStack() as ctx:
         pool = ctx.enter_context(tc.tile_pool(name="held", bufs=1))
         psum = ctx.enter_context(tc.psum_pool(name="psum", bufs=1))
 
-        pool_scales = pool.tile([P, T], U8, name="pool_scales", align_bytes=64)
-        nc.vector.memset(pool_scales[:].bitcast(I32), 0)
-        slot_list = pool.tile([P, SLOTS // 16], U16, name="slot_list")
-        nc.sync.dma_start(slot_list[:], offs)
-        pool_words = pool.tile([P, T], U32, name="pool_words", align_bytes=64)
+        store_scales = pool.tile([P, TOKENS], U8, name="store_scales", align_bytes=64)
+        nc.vector.memset(store_scales[:].bitcast(I32), 0)
+        store_words = pool.tile([P, TOKENS], U32, name="store_words", align_bytes=64)
         words_in = keys_words[0].rearrange("p n t -> p (n t)").bitcast(I32)
-        nc.sync.dma_start(out=pool_words[:, 0:HEAD].bitcast(I32), in_=words_in[:, 0:HEAD])
-        for r in range(4):
+        nc.sync.dma_start(out=store_words[:, 0:HEAD].bitcast(I32), in_=words_in[:, 0:HEAD])
+        slot_list = pool.tile([P, SLOTS // LIST_ROWS], U16, name="slot_list")
+        nc.sync.dma_start(slot_list[:], offs)
+        for r in range(SCALE_ROWS):
             nc.sync.dma_start(
-                out=pool_scales[r:P:32, :].bitcast(I32), in_=keys_scales[0][r:16:4, :].bitcast(I32)
+                out=store_scales[r:P:QUADRANT, :].bitcast(I32),
+                in_=keys_scales[0][r : D // 32 : SCALE_ROWS, :].bitcast(I32),
             )
-        nc.sync.dma_start(out=pool_words[:, HEAD:T].bitcast(I32), in_=words_in[:, HEAD:T])
+        nc.sync.dma_start(out=store_words[:, HEAD:TOKENS].bitcast(I32), in_=words_in[:, HEAD:TOKENS])
         q_raw = load_rows(nc, pool, query, "q_raw", "key_words1")
         pg_raw = [load_rows(nc, pool, pgsum[:, h * HALF : (h + 1) * HALF], f"pg_raw{h}") for h in range(2)]
         pq_raw = load_rows(nc, pool, pquery, "pq_raw")
-        page_list = pool.tile([P, PAGES // 16], U16, name="page_list")
+        page_list = pool.tile([P, PAGES // LIST_ROWS], U16, name="page_list")
         nc.sync.dma_start(page_list[:], offs2)
 
-        placed = pool.tile([P, U], F32, name="placed")
-        nc.gpsimd.memset(placed[:], 0.0)
+        placed = pool.tile([P, ALL_PAGES], F32, name="placed")
+        nc.vector.memset(placed[:], 0.0)
 
-        q_bf = pool.tile([P, Q, PACK], BF16, name="q_bf", align_bytes=64)
-        interleave(nc, q_bf[:], q_raw)
+        q_bf = pool.tile([P, ROWS, PACK], BF16, name="q_bf", align_bytes=64)
+        interleave_on_scalar(nc, q_bf, q_raw)
         key_scales = pool.tile([P, SLOTS], U8, name="key_scales", align_bytes=64)
-        nc.vector.tensor_copy(key_scales[:], pool_scales[:].indirect(slot_list[:]))
+        nc.vector.tensor_copy(key_scales[:], store_scales[:].indirect(slot_list[:]))
+
+        def gather_words(c):
+            key_words = pool.tile([P, CHUNK], U32, name=f"key_words{c}", tag=f"key_words{c}", align_bytes=64)
+            entries = slot_list[:, c * CHUNK // LIST_ROWS : (c + 1) * CHUNK // LIST_ROWS]
+            nc.vector.tensor_copy(key_words[:], store_words[:].indirect(entries))
+            return key_words
 
         scores = []
-        for c in range(CHUNKS):
-            key_words = pool.tile([P, CHUNK], U32, name=f"key_words{c}", tag=f"key_words{c}", align_bytes=64)
-            cols = slice(c * CHUNK // 16, (c + 1) * CHUNK // 16)
-            nc.vector.tensor_copy(key_words[:], pool_words[:].indirect(slot_list[:, cols]))
-            if c == 0:
-                q_codes, q_scales = quantise(nc, pool, q_bf, "q")
+
+        def score(c, key_words):
             for h in range(CHUNK // PIECE):
                 bank = psum.tile([P, PIECE], F32, name=f"scores{c}{h}")
-                nc.tensor.matmul_mx(
-                    out=bank[:],
-                    lhsT=q_codes[:].bitcast(FP8X4),
-                    lhsT_scale=q_scales[:],
-                    rhs=key_words[:, h * PIECE : (h + 1) * PIECE].bitcast(FP8X4),
-                    rhs_scale=key_scales[:, c * CHUNK + h * PIECE : c * CHUNK + (h + 1) * PIECE],
-                    start=True,
-                    stop=True,
+                first = c * CHUNK + h * PIECE
+                multiply(
+                    nc, bank, q_codes, q_scales,
+                    key_words[:, h * PIECE : (h + 1) * PIECE], key_scales[:, first : first + PIECE],
                 )
                 scores.append(bank[:].rearrange("p (g j) -> p g j", j=PAGE))
 
-        pq_bf = pool.tile([P, Q, PACK], BF16, name="pq_bf", align_bytes=64)
+        first_words = gather_words(0)
+        q_codes, q_scales = quantise(nc, pool, q_bf, "q")
+        score(0, first_words)
+        score(1, gather_words(1))
+
+        pq_bf = pool.tile([P, ROWS, PACK], BF16, name="pq_bf", align_bytes=64)
         pg_bf = [pool.tile([P, HALF, PACK], BF16, name=f"pg_bf{h}", align_bytes=64) for h in range(2)]
-        interleave(nc, pg_bf[0][:], pg_raw[0])
-        for grouped, raw in ((pg_bf[1], pg_raw[1]), (pq_bf, pq_raw)):
-            nc.gpsimd.tensor_scalar(
-                out=grouped[:],
-                in0=raw[:].rearrange("p t c -> p c t"),
-                scalar1=1.0,
-                scalar2=0.0,
-                op0=ALU.mult,
-                op1=ALU.add,
-            )
+        interleave_on_scalar(nc, pg_bf[0], pg_raw[0])
+        interleave_on_gpsimd(nc, pg_bf[1], pg_raw[1])
+        interleave_on_gpsimd(nc, pq_bf, pq_raw)
 
         top = pool.tile([P, PAGES], F32, name="top")
         total = pool.tile([P, PAGES], F32, name="total")
@@ -139,6 +161,10 @@ def tile_attend_pagelogsum_kernel(tc, query, keys_words, keys_scales, pquery, pg
             )
             nc.scalar.activation(out=power[:, pages(n), :], in_=shifted[:], func=ACT.Exp)
 
+        def add_up(c):
+            chunk_pages = slice(c * CHUNK_PAGES, (c + 1) * CHUNK_PAGES)
+            nc.vector.tensor_reduce(out=total[:, chunk_pages], in_=power[:, chunk_pages, :], axis=AX.X, op=ALU.add)
+
         nc.vector.tensor_reduce(out=minus_top[:], in_=scores[0], axis=AX.X, op=ALU.max, negate=True)
         for g in range(PIECE_PAGES):
             nc.scalar.activation(
@@ -154,26 +180,14 @@ def tile_attend_pagelogsum_kernel(tc, query, keys_words, keys_scales, pquery, pg
             out=top[:, pages(0)], in0=minus_top[:], scalar1=-1.0, scalar2=None, op0=ALU.mult
         )
 
-        nc.vector.tensor_reduce(
-            out=total[:, 0:CHUNK_PAGES], in_=power[:, 0:CHUNK_PAGES, :], axis=AX.X, op=ALU.add
-        )
+        add_up(0)
         pq_codes, pq_scales = quantise(nc, pool, pq_bf, "pq")
-        nc.vector.tensor_reduce(
-            out=total[:, CHUNK_PAGES:PAGES], in_=power[:, CHUNK_PAGES:PAGES, :], axis=AX.X, op=ALU.add
-        )
+        add_up(1)
         summary = []
         for h in range(2):
             pg_codes, pg_scales = quantise(nc, pool, pg_bf[h], f"pg{h}")
             bank = psum.tile([P, HALF], F32, name=f"summary{h}")
-            nc.tensor.matmul_mx(
-                out=bank[:],
-                lhsT=pq_codes[:].bitcast(FP8X4),
-                lhsT_scale=pq_scales[:],
-                rhs=pg_codes[:].bitcast(FP8X4),
-                rhs_scale=pg_scales[:],
-                start=True,
-                stop=True,
-            )
+            multiply(nc, bank, pq_codes, pq_scales, pg_codes[:], pg_scales[:])
             summary.append(bank)
 
         logs = pool.tile([P, PAGES], F32, name="logs")

from contextlib import ExitStack

import concourse.mybir as mybir

D, TOKENS, SLOTS, PAGES, ALL_PAGES, ROWS = 512, 4096, 1024, 64, 512, 128
FLOPS = 2 * D * ROWS * (SLOTS + ALL_PAGES)

F32 = mybir.dt.float32
BF16 = mybir.dt.bfloat16
I32 = mybir.dt.int32
U32 = mybir.dt.uint32
U16 = mybir.dt.uint16
U8 = mybir.dt.uint8
FP8X4 = mybir.dt.float8_e4m3fn_x4
ALU = mybir.AluOpType
ACT = mybir.ActivationFunctionType
AX = mybir.AxisListType

P = 128
PACK = 4
LIST_ROWS = 16
QUADRANT = 32
SCALE_ROWS = 4
LINE = 4
PAGE = SLOTS // PAGES
CHUNK = 512
CHUNK_PAGES = CHUNK // PAGE
PIECE = 256
PIECE_PAGES = PIECE // PAGE
HALF = ALL_PAGES // 2
HEAD = 1280


def load_rows(nc, pool, src, name, tag=None):
    width = src.shape[1]
    raw = pool.tile([P, PACK, width], F32, name=name, tag=tag or name, align_bytes=64)
    nc.sync.dma_start(out=raw[:], in_=src.rearrange("(p t) c -> p t c", t=PACK))
    return raw


def interleave_on_scalar(nc, grouped, raw):
    nc.scalar.copy(
        out=grouped[:].rearrange("p (c i) t -> p c t i", i=LINE),
        in_=raw[:].rearrange("p t (c i) -> p c t i", i=LINE),
    )


def interleave_on_gpsimd(nc, grouped, raw):
    nc.gpsimd.tensor_scalar(
        out=grouped[:],
        in0=raw[:].rearrange("p t c -> p c t"),
        scalar1=1.0,
        scalar2=0.0,
        op0=ALU.mult,
        op1=ALU.add,
    )


def quantise(nc, pool, grouped, name):
    width = grouped.shape[1]
    codes = pool.tile([P, width], U32, name=name + "_codes", align_bytes=64)
    scales = pool.tile([P, width], U8, name=name + "_scales", align_bytes=64)
    nc.vector.quantize_mx(
        out=codes[:].bitcast(FP8X4), scales=scales[:], in_=grouped[:].rearrange("p c t -> p (c t)")
    )
    return codes, scales


def multiply(nc, bank, row_codes, row_scales, codes, scales):
    nc.tensor.matmul_mx(
        out=bank[:],
        lhsT=row_codes[:].bitcast(FP8X4),
        lhsT_scale=row_scales[:],
        rhs=codes.bitcast(FP8X4),
        rhs_scale=scales,
        start=True,
        stop=True,
    )


def tile_attend_pagelogsum_kernel(tc, query, keys_words, keys_scales, pquery, pgsum, offs, offs2, out):
    nc = tc.nc
    with ExitStack() as ctx:
        pool = ctx.enter_context(tc.tile_pool(name="held", bufs=1))
        psum = ctx.enter_context(tc.psum_pool(name="psum", bufs=1))

        store_scales = pool.tile([P, TOKENS], U8, name="store_scales", align_bytes=64)
        nc.vector.memset(store_scales[:].bitcast(I32), 0)
        store_words = pool.tile([P, TOKENS], U32, name="store_words", align_bytes=64)
        words_in = keys_words[0].rearrange("p n t -> p (n t)").bitcast(I32)
        nc.sync.dma_start(out=store_words[:, 0:HEAD].bitcast(I32), in_=words_in[:, 0:HEAD])
        slot_list = pool.tile([P, SLOTS // LIST_ROWS], U16, name="slot_list")
        nc.sync.dma_start(slot_list[:], offs)
        for r in range(SCALE_ROWS):
            nc.sync.dma_start(
                out=store_scales[r:P:QUADRANT, :].bitcast(I32),
                in_=keys_scales[0][r : D // 32 : SCALE_ROWS, :].bitcast(I32),
            )
        nc.sync.dma_start(out=store_words[:, HEAD:TOKENS].bitcast(I32), in_=words_in[:, HEAD:TOKENS])
        q_raw = load_rows(nc, pool, query, "q_raw", "key_words1")
        pg_raw = [load_rows(nc, pool, pgsum[:, h * HALF : (h + 1) * HALF], f"pg_raw{h}") for h in range(2)]
        pq_raw = load_rows(nc, pool, pquery, "pq_raw")
        page_list = pool.tile([P, PAGES // LIST_ROWS], U16, name="page_list")
        nc.sync.dma_start(page_list[:], offs2)

        placed = pool.tile([P, ALL_PAGES], F32, name="placed")
        nc.vector.memset(placed[:], 0.0)

        q_bf = pool.tile([P, ROWS, PACK], BF16, name="q_bf", align_bytes=64)
        interleave_on_scalar(nc, q_bf, q_raw)
        key_scales = pool.tile([P, SLOTS], U8, name="key_scales", align_bytes=64)
        nc.vector.tensor_copy(key_scales[:], store_scales[:].indirect(slot_list[:]))

        def gather_words(c):
            key_words = pool.tile([P, CHUNK], U32, name=f"key_words{c}", tag=f"key_words{c}", align_bytes=64)
            entries = slot_list[:, c * CHUNK // LIST_ROWS : (c + 1) * CHUNK // LIST_ROWS]
            nc.vector.tensor_copy(key_words[:], store_words[:].indirect(entries))
            return key_words

        scores = []

        def score(c, key_words):
            for h in range(CHUNK // PIECE):
                bank = psum.tile([P, PIECE], F32, name=f"scores{c}{h}")
                first = c * CHUNK + h * PIECE
                multiply(
                    nc, bank, q_codes, q_scales,
                    key_words[:, h * PIECE : (h + 1) * PIECE], key_scales[:, first : first + PIECE],
                )
                scores.append(bank[:].rearrange("p (g j) -> p g j", j=PAGE))

        first_words = gather_words(0)
        q_codes, q_scales = quantise(nc, pool, q_bf, "q")
        score(0, first_words)
        score(1, gather_words(1))

        pq_bf = pool.tile([P, ROWS, PACK], BF16, name="pq_bf", align_bytes=64)
        pg_bf = [pool.tile([P, HALF, PACK], BF16, name=f"pg_bf{h}", align_bytes=64) for h in range(2)]
        interleave_on_scalar(nc, pg_bf[0], pg_raw[0])
        interleave_on_gpsimd(nc, pg_bf[1], pg_raw[1])
        interleave_on_gpsimd(nc, pq_bf, pq_raw)

        top = pool.tile([P, PAGES], F32, name="top")
        total = pool.tile([P, PAGES], F32, name="total")
        power = pool.tile([P, PAGES, PAGE], F32, name="power")
        minus_top = pool.tile([P, PIECE_PAGES], F32, name="minus_top")

        def pages(n):
            return slice(n * PIECE_PAGES, (n + 1) * PIECE_PAGES)

        def find_top(n):
            nc.vector.tensor_reduce(out=top[:, pages(n)], in_=scores[n], axis=AX.X, op=ALU.max)

        def exponentials(n):
            shifted = pool.tile([P, PIECE_PAGES, PAGE], F32, name=f"shifted{n}")
            nc.vector.tensor_tensor(
                out=shifted[:],
                in0=scores[n],
                in1=top[:, pages(n)].unsqueeze(2).to_broadcast([P, PIECE_PAGES, PAGE]),
                op=ALU.subtract,
            )
            nc.scalar.activation(out=power[:, pages(n), :], in_=shifted[:], func=ACT.Exp)

        def add_up(c):
            chunk_pages = slice(c * CHUNK_PAGES, (c + 1) * CHUNK_PAGES)
            nc.vector.tensor_reduce(out=total[:, chunk_pages], in_=power[:, chunk_pages, :], axis=AX.X, op=ALU.add)

        nc.vector.tensor_reduce(out=minus_top[:], in_=scores[0], axis=AX.X, op=ALU.max, negate=True)
        for g in range(PIECE_PAGES):
            nc.scalar.activation(
                out=power[:, g, :], in_=scores[0][:, g, :], func=ACT.Exp, bias=minus_top[:, g : g + 1]
            )
        find_top(1)
        find_top(2)
        exponentials(1)
        find_top(3)
        exponentials(2)
        exponentials(3)
        nc.vector.tensor_scalar(
            out=top[:, pages(0)], in0=minus_top[:], scalar1=-1.0, scalar2=None, op0=ALU.mult
        )

        add_up(0)
        pq_codes, pq_scales = quantise(nc, pool, pq_bf, "pq")
        add_up(1)
        summary = []
        for h in range(2):
            pg_codes, pg_scales = quantise(nc, pool, pg_bf[h], f"pg{h}")
            bank = psum.tile([P, HALF], F32, name=f"summary{h}")
            multiply(nc, bank, pq_codes, pq_scales, pg_codes[:], pg_scales[:])
            summary.append(bank)

        logs = pool.tile([P, PAGES], F32, name="logs")
        nc.scalar.activation(out=logs[:], in_=total[:], func=ACT.Ln)
        nc.vector.tensor_tensor(placed[:].indirect(page_list[:]), logs[:], top[:], ALU.add)

        for h, queue in enumerate((nc.sync, nc.scalar)):
            cols = slice(h * HALF, (h + 1) * HALF)
            result = pool.tile([P, HALF], F32, name=f"result{h}")
            nc.vector.tensor_tensor(out=result[:], in0=summary[h][:], in1=placed[:, cols], op=ALU.add)
            queue.dma_start(out=out[:, cols], in_=result[:])
